import numpy as np
import ml_dtypes


def mxq(x, axis, fmt="e4m3"):
    dtype, down = {"e4m3": (ml_dtypes.float8_e4m3fn, 7), "e5m2": (ml_dtypes.float8_e5m2, 14)}[fmt]
    v = np.moveaxis(np.asarray(x, np.float32).astype(ml_dtypes.bfloat16).astype(np.float64), axis, -1)
    blocks = v.reshape(v.shape[:-1] + (-1, 32))
    amax = np.abs(blocks).max(-1, keepdims=True)
    byte = np.maximum(np.where(amax > 0, np.frexp(amax)[1] - 1 + 127, 0) - down, 1)
    scale = np.exp2(byte - 127.0)
    codes = (blocks / scale).astype(np.float32).astype(dtype).astype(np.float64)
    return np.moveaxis((codes * scale).reshape(v.shape), -1, axis)


WIDE = False


def mx_kscale(k):
    if not WIDE:
        return np.ones(k)
    levels = np.array([10, -10, 5, -5, 0])
    if k % 512:
        return np.exp2(np.random.permutation(np.resize(levels, k // 32))).repeat(32)
    a = np.empty((k // 512, 16))
    for p in range(k // 512):
        a[p, :8] = np.random.permutation(np.resize(levels, 8))
        for g in range(8):
            far = levels[np.abs(levels - a[p, g]) >= 10]
            a[p, g + 8] = far[np.random.randint(len(far))]
    return np.exp2(a.ravel()).repeat(32)


def f64(x):
    return np.asarray(x).astype(np.float64)


E2M1 = np.array([0.0, 0.5, 1.0, 1.5, 2.0, 3.0, 4.0, 6.0, -0.0, -0.5, -1.0, -1.5, -2.0, -3.0, -4.0, -6.0])


def pack_weight(w, fmt):
    k, n = w.shape
    w = f64(np.asarray(w, np.float32).astype(ml_dtypes.bfloat16)).reshape(k // 32, 32, n)
    amax = np.abs(w).max(1)
    if fmt == "e4m3":
        byte = np.frexp(amax)[1] - 1 + 127 - 7
    else:
        mant, ex = np.frexp(amax / 6.0)
        byte = np.where(mant > 0.5, ex, ex - 1) + 127
    byte = np.clip(np.where(amax > 0, byte, 1), 1, 254)
    scaled = (w * np.exp2(127.0 - byte)[:, None, :]).reshape(k, n).astype(np.float32)
    by_word = np.ascontiguousarray(scaled.reshape(k // 512, 128, 4, n).transpose(0, 1, 3, 2))
    if fmt == "e4m3":
        words = by_word.astype(ml_dtypes.float8_e4m3fn).view(np.uint8)
    else:
        c = by_word.astype(ml_dtypes.float4_e2m1fn).view(np.uint8) & 0xF
        words = (c[..., 0::2] | (c[..., 1::2] << 4)).reshape(k // 512, 128, 2 * n)
    return np.ascontiguousarray(words), np.ascontiguousarray(byte.astype(np.uint8).reshape(k // 512, 16, n))


def unpack_weight(words, scales, fmt):
    g, _, n = scales.shape
    words = np.ascontiguousarray(words).reshape(g, 128, n, -1)
    if fmt == "e4m3":
        vals = words.view(ml_dtypes.float8_e4m3fn).astype(np.float64)
    else:
        nib = np.empty((g, 128, n, 4), np.uint8)
        nib[..., 0::2] = words & 0xF
        nib[..., 1::2] = words >> 4
        vals = E2M1[nib]
    vals = vals * np.repeat(np.exp2(scales.astype(np.float64) - 127.0), 8, axis=1)[..., None]
    return vals.transpose(0, 1, 3, 2).reshape(g * 512, n)


def sigmoid(v):
    return 1.0 / (1.0 + np.exp(-v))


K, L, T, R, N = 1024, 512, 512, 512, 512


def setup_inputs():
    n = np.random.standard_normal
    fk = mx_kscale(K)
    fl = mx_kscale(L)
    fr = mx_kscale(R)
    xtp = pack_weight(n((K, T)) / fk[:, None], "e4m3")
    wap = pack_weight(n((K, R)) * 1 / np.sqrt(K) * fk[:, None], "e2m1")
    xqp = pack_weight(n((L, T)) / fl[:, None], "e4m3")
    wcp = pack_weight(n((L, R)) * 1 / np.sqrt(L) * fl[:, None], "e2m1")
    wgp = pack_weight(n((L, R)) * 1 / np.sqrt(L) * fl[:, None], "e4m3")
    wbp = pack_weight(n((R, N)) * 1 / np.sqrt(R) / fr[:, None], "e2m1")
    wqp = pack_weight(n((L, N)) * 1 / np.sqrt(L) * fl[:, None], "e4m3")
    return {
        "xt_words": xtp[0],
        "xt_scales": xtp[1],
        "wa_words": wap[0],
        "wa_scales": wap[1],
        "xq_words": xqp[0],
        "xq_scales": xqp[1],
        "wc_words": wcp[0],
        "wc_scales": wcp[1],
        "wg_words": wgp[0],
        "wg_scales": wgp[1],
        "us": (np.random.uniform(0.5, 2.0, (R, 1)) * fr[:, None]).astype(np.float32),
        "wb_words": wbp[0],
        "wb_scales": wbp[1],
        "wq_words": wqp[0],
        "wq_scales": wqp[1],
    }


def reference(xt_words, xt_scales, wa_words, wa_scales, xq_words, xq_scales, wc_words, wc_scales, wg_words, wg_scales, us, wb_words, wb_scales, wq_words, wq_scales):
    xtu = unpack_weight(xt_words, xt_scales, "e4m3")
    wau = unpack_weight(wa_words, wa_scales, "e2m1")
    xqu = unpack_weight(xq_words, xq_scales, "e4m3")
    wcu = unpack_weight(wc_words, wc_scales, "e2m1")
    wgu = unpack_weight(wg_words, wg_scales, "e4m3")
    wbu = unpack_weight(wb_words, wb_scales, "e2m1")
    wqu = unpack_weight(wq_words, wq_scales, "e4m3")
    z = wau.T @ xtu + wcu.T @ xqu
    g = wgu.T @ xqu
    hid = z * sigmoid(g) * f64(us)
    hidq = mxq(hid, 0, "e4m3")
    y = wbu.T @ hidq + wqu.T @ xqu
    return y

@@ -1,0 +1,240 @@
+from contextlib import ExitStack
+
+import concourse.mybir as mybir
+from concourse.masks import make_identity
+
+K, L, T, R, N = 1024, 512, 512, 512, 512
+FLOPS = 2 * T * (K * R + 2 * L * R + R * N + L * N)
+
+F32 = mybir.dt.float32
+BF16 = mybir.dt.bfloat16
+I32 = mybir.dt.int32
+U8 = mybir.dt.uint8
+FP8X4 = mybir.dt.float8_e4m3fn_x4
+FP4X4 = mybir.dt.float4_e2m1fn_x4
+ACT = mybir.ActivationFunctionType
+ALU = mybir.AluOpType
+
+P = 128
+W = 512
+TILES = T // P
+
+
+def tile_mix_hidden_of_two_inputs_gated_kernel(
+    tc, xt_words, xt_scales, wa_words, wa_scales, xq_words, xq_scales, wc_words, wc_scales,
+    wg_words, wg_scales, us, wb_words, wb_scales, wq_words, wq_scales, out,
+):
+    nc = tc.nc
+    with ExitStack() as ctx:
+        keep = ctx.enter_context(tc.tile_pool(name="keep", bufs=1))
+        work = ctx.enter_context(tc.tile_pool(name="work", bufs=4))
+        psum = ctx.enter_context(tc.psum_pool(name="psum", bufs=1))
+        ctx.enter_context(tc.manual_schedule())
+
+        def load_rows(engine, stage, first, scales):
+            passes = scales.shape[0]
+            dst = stage[4:P:8, first * W : (first + passes) * W].bitcast(I32)
+            engine.dma_start(
+                out=dst.rearrange("q (z c) -> q z c", z=passes),
+                in_=scales.rearrange("z q c -> q z c").bitcast(I32),
+            )
+
+        def place_rows(engine, planes, stage):
+            for q in range(4):
+                engine.dma_start(
+                    out=planes[32 * q : 32 * q + 4, :].bitcast(I32),
+                    in_=stage[32 * q + 4 : 32 * q + 32 : 8, :].bitcast(I32),
+                )
+
+        def load_fp8(words, name):
+            tl = keep.tile([P, W], I32, name=name, align_bytes=64)
+            nc.sync.dma_start(out=tl[:], in_=words.rearrange("p c r -> p (c r)").bitcast(I32))
+            return tl
+
+        def load_fp4(words, name):
+            tl = keep.tile([P, 2 * W], U8, name=name, align_bytes=64)
+            nc.sync.dma_start(out=tl[:].bitcast(I32), in_=words.bitcast(I32))
+            return tl
+
+        stage1 = keep.tile([P, 7 * W], U8, align_bytes=64)
+        planes1 = keep.tile([P, 7 * W], U8, align_bytes=64)
+        stage2 = keep.tile([P, 2 * W], U8, align_bytes=64)
+        planes2 = keep.tile([P, 2 * W], U8, align_bytes=64)
+        us_col = keep.tile([P, 4], F32)
+        ident = keep.tile([P, P], F32, align_bytes=64)
+        warm = keep.tile([P, 1], F32)
+        warm_out = keep.tile([P, 1], F32)
+
+        load_rows(nc.sync, stage1, 0, xq_scales)
+        load_rows(nc.sync, stage1, 1, wg_scales)
+        load_rows(nc.sync, stage1, 2, wc_scales)
+        load_rows(nc.sync, stage1, 3, wa_scales)
+        load_rows(nc.sync, stage1, 5, xt_scales)
+        xq = load_fp8(xq_words[0], "xq")
+        wg = load_fp8(wg_words[0], "wg")
+        wc = load_fp4(wc_words[0], "wc")
+
+        nc.gpsimd.dma_start(out=us_col[:], in_=us.rearrange("(p j) o -> p (j o)", j=4))
+        make_identity(nc, ident[:])
+        load_rows(nc.gpsimd, stage2, 0, wq_scales)
+        load_rows(nc.gpsimd, stage2, 1, wb_scales)
+
+        nc.vector.memset(warm[:], 0.0)
+        nc.vector.memset(planes1[:].bitcast(I32), 0)
+        nc.vector.memset(planes2[:].bitcast(I32), 0)
+        nc.scalar.activation(out=warm_out[:], in_=warm[:], func=ACT.Sigmoid)
+        place_rows(nc.scalar, planes1, stage1)
+
+        wa = keep.tile([P, 2, 2 * W], U8, align_bytes=64)
+        nc.sync.dma_start(out=wa[:].bitcast(I32), in_=wa_words.rearrange("z p b -> p z b").bitcast(I32))
+        xt = [load_fp8(xt_words[z], "xt%d" % z) for z in range(2)]
+        wq = load_fp8(wq_words[0], "wq")
+        wb = load_fp4(wb_words[0], "wb")
+        place_rows(nc.sync, planes2, stage2)
+
+        def plane1(a, cols):
+            return planes1[:, a * W + cols.start : a * W + cols.stop]
+
+        every = slice(0, W)
+        us_row = psum.tile([P, 4, P], F32, tag="o", bufs=3, name="us_row")
+        for j in range(4):
+            nc.tensor.transpose(us_row[:, j, :], us_col[:, j : j + 1].to_broadcast([P, P]), ident[:])
+
+        gate, zsum, sig, fac, hid, turned, grouped, codes, cscale, acc = ({} for i in range(10))
+
+        def toks(i):
+            return slice(i * P, (i + 1) * P)
+
+        def gate_pass(i):
+            gate[i] = psum.tile([P, W], F32, tag="g", bufs=2, name="gate")
+            nc.tensor.matmul_mx(
+                out=gate[i][:], lhsT=xq[:, toks(i)].bitcast(FP8X4), lhsT_scale=plane1(0, toks(i)),
+                rhs=wg[:].bitcast(FP8X4), rhs_scale=plane1(1, every), start=True, stop=True,
+            )
+
+        def z_pass(i, s):
+            if s == 0:
+                zsum[i] = psum.tile([P, W], F32, tag="z", bufs=3, name="zsum")
+                x, xs, w, ws = xq, 0, wc[:], 2
+            else:
+                x, xs, w, ws = xt[s - 1], 4 + s, wa[:, s - 1, :], 2 + s
+            nc.tensor.matmul_mx(
+                out=zsum[i][:], lhsT=x[:, toks(i)].bitcast(FP8X4), lhsT_scale=plane1(xs, toks(i)),
+                rhs=w.bitcast(FP4X4), rhs_scale=plane1(ws, every), start=(s == 0), stop=(s == 2),
+            )
+
+        def sigmoid(i):
+            sig[i] = work.tile([P, 2, P, 2], F32, name="sig")
+            nc.scalar.activation(
+                out=sig[i][:], in_=gate[i][:].rearrange("t (p u e) -> t u p e", u=2, e=2), func=ACT.Sigmoid
+            )
+
+        def factor(i):
+            fac[i] = work.tile([P, 2, P, 2], F32, name="fac")
+            nc.vector.tensor_tensor(
+                out=fac[i][:], in0=sig[i][:], in1=us_row[:].rearrange("t (u e) p -> t u p e", e=2), op=ALU.mult
+            )
+
+        def hidden(i):
+            hid[i] = work.tile([P, 2, P, 2], BF16, name="hid", align_bytes=64)
+            nc.vector.tensor_tensor(
+                out=hid[i][:], in0=zsum[i][:].rearrange("t (p u e) -> t u p e", u=2, e=2), in1=fac[i][:], op=ALU.mult
+            )
+
+        def turn(i):
+            turned[i] = psum.tile([P, 2, P], F32, tag="g", bufs=2, name="turned")
+            pairs = hid[i][:].rearrange("t u p e -> t (u p e)").bitcast(F32)
+            for u in range(2):
+                nc.tensor.transpose(turned[i][:, u, :], pairs[:, u * P : (u + 1) * P], ident[:])
+
+        def regroup(i):
+            grouped[i] = work.tile([P, 4 * P], BF16, name="grouped", align_bytes=64)
+            nc.scalar.copy(
+                out=grouped[i][:].bitcast(F32).rearrange("p (t u) -> p t u", u=2),
+                in_=turned[i][:].rearrange("p u t -> p t u"),
+            )
+
+        def quantise(i):
+            codes[i] = work.tile([P, P], I32, name="codes", align_bytes=64)
+            cscale[i] = work.tile([P, P], U8, name="cscale", align_bytes=64)
+            nc.vector.quantize_mx(out=codes[i][:].bitcast(FP8X4), scales=cscale[i][:], in_=grouped[i][:])
+
+        def skip_passes(i, rows, tag):
+            acc[i, rows] = psum.tile([P, len(rows), P], F32, tag=tag, bufs=3, name="acc")
+            for b, a in enumerate(rows):
+                nc.tensor.matmul_mx(
+                    out=acc[i, rows][:, b, :], lhsT=wq[:, toks(a)].bitcast(FP8X4), lhsT_scale=planes2[:, toks(a)],
+                    rhs=xq[:, toks(i)].bitcast(FP8X4), rhs_scale=plane1(0, toks(i)), start=(b == 0), stop=False,
+                )
+
+        def second_passes(i, rows):
+            for b, a in enumerate(rows):
+                nc.tensor.matmul_mx(
+                    out=acc[i, rows][:, b, :], lhsT=wb[:, 2 * a * P : 2 * (a + 1) * P].bitcast(FP4X4),
+                    lhsT_scale=planes2[:, W + a * P : W + (a + 1) * P],
+                    rhs=codes[i][:].bitcast(FP8X4), rhs_scale=cscale[i][:], start=False, stop=(b == len(rows) - 1),
+                )
+
+        def leave(i, rows, engine):
+            res = work.tile([P, len(rows), P], F32, name="res", bufs=5)
+            if engine == "scalar":
+                nc.scalar.copy(out=res[:], in_=acc[i, rows][:])
+            else:
+                nc.vector.tensor_copy(out=res[:], in_=acc[i, rows][:])
+            dst = out.rearrange("(a p) t -> p a t", p=P)[:, rows[0] : rows[-1] + 1, toks(i)]
+            nc.sync.dma_start(out=dst, in_=res[:])
+
+        gate_pass(0)
+        sigmoid(0)
+        gate_pass(1)
+        sigmoid(1)
+        z_pass(0, 0)
+        z_pass(1, 0)
+        factor(0)
+        factor(1)
+        z_pass(0, 1)
+        z_pass(0, 2)
+        hidden(0)
+        gate_pass(2)
+        sigmoid(2)
+        z_pass(1, 1)
+        z_pass(1, 2)
+        hidden(1)
+        gate_pass(3)
+        sigmoid(3)
+        factor(2)
+        factor(3)
+        for s in range(3):
+            z_pass(2, s)
+        hidden(2)
+        turn(0)
+        regroup(0)
+        turn(1)
+        regroup(1)
+        quantise(0)
+        for s in range(3):
+            z_pass(3, s)
+        hidden(3)
+        quantise(1)
+        whole, low, high = (0, 1, 2, 3), (0, 1), (2, 3)
+        skip_passes(0, whole, "o")
+        second_passes(0, whole)
+        turn(2)
+        regroup(2)
+        turn(3)
+        regroup(3)
+        leave(0, whole, "scalar")
+        quantise(2)
+        quantise(3)
+        skip_passes(1, whole, "o")
+        second_passes(1, whole)
+        leave(1, whole, "vector")
+        skip_passes(2, whole, "o")
+        second_passes(2, whole)
+        leave(2, whole, "scalar")
+        skip_passes(3, low, "z")
+        second_passes(3, low)
+        leave(3, low, "vector")
+        skip_passes(3, high, "z")
+        second_passes(3, high)
+        leave(3, high, "scalar")

@@ -46,9 +46,9 @@ def tile_mix_hidden_of_two_inputs_gated_kernel(
                     in_=stage[32 * q + 4 : 32 * q + 32 : 8, :].bitcast(I32),
                 )
 
-        def load_fp8(words, name):
+        def load_fp8(words, name, engine=nc.sync):
             tl = keep.tile([P, W], I32, name=name, align_bytes=64)
-            nc.sync.dma_start(out=tl[:], in_=words.rearrange("p c r -> p (c r)").bitcast(I32))
+            engine.dma_start(out=tl[:], in_=words.rearrange("p c r -> p (c r)").bitcast(I32))
             return tl
 
         def load_fp4(words, name):
@@ -65,32 +65,48 @@ def tile_mix_hidden_of_two_inputs_gated_kernel(
         warm = keep.tile([P, 1], F32)
         warm_out = keep.tile([P, 1], F32)
 
+        ones = keep.tile([P, 4 * P], BF16, align_bytes=64)
+        ones_codes = keep.tile([P, P], I32, align_bytes=64)
+        ones_scale = keep.tile([P, P], U8, align_bytes=64)
+
         load_rows(nc.sync, stage1, 0, xq_scales)
-        load_rows(nc.sync, stage1, 1, wg_scales)
+        load_rows(nc.scalar, stage1, 1, wg_scales)
         load_rows(nc.sync, stage1, 2, wc_scales)
-        load_rows(nc.sync, stage1, 3, wa_scales)
+        load_rows(nc.scalar, stage1, 3, wa_scales)
         load_rows(nc.sync, stage1, 5, xt_scales)
-        xq = load_fp8(xq_words[0], "xq")
-        wg = load_fp8(wg_words[0], "wg")
-        wc = load_fp4(wc_words[0], "wc")
+        xq = load_fp8(xq_words[0], "xq", nc.scalar)
+        wg = load_fp8(wg_words[0], "wg", nc.scalar)
+        xt_both = keep.tile([P, 2, W], I32, align_bytes=64)
+        nc.scalar.dma_start(out=xt_both[:], in_=xt_words.rearrange("z p c r -> p z (c r)").bitcast(I32))
+        xt = [xt_both[:, z, :] for z in range(2)]
 
         nc.gpsimd.dma_start(out=us_col[:], in_=us.rearrange("(p j) o -> p (j o)", j=4))
         make_identity(nc, ident[:])
         load_rows(nc.gpsimd, stage2, 0, wq_scales)
         load_rows(nc.gpsimd, stage2, 1, wb_scales)
 
+        nc.vector.memset(ones[:], 1.0)
         nc.vector.memset(warm[:], 0.0)
+        nc.vector.quantize_mx(out=ones_codes[:].bitcast(FP8X4), scales=ones_scale[:], in_=ones[:])
         nc.vector.memset(planes1[:].bitcast(I32), 0)
         nc.vector.memset(planes2[:].bitcast(I32), 0)
         nc.scalar.activation(out=warm_out[:], in_=warm[:], func=ACT.Sigmoid)
-        place_rows(nc.scalar, planes1, stage1)
+        place_rows(nc.sync, planes1, stage1)
 
         wa = keep.tile([P, 2, 2 * W], U8, align_bytes=64)
         nc.sync.dma_start(out=wa[:].bitcast(I32), in_=wa_words.rearrange("z p b -> p z b").bitcast(I32))
-        xt = [load_fp8(xt_words[z], "xt%d" % z) for z in range(2)]
+        wc = load_fp4(wc_words[0], "wc")
         wq = load_fp8(wq_words[0], "wq")
         wb = load_fp4(wb_words[0], "wb")
         place_rows(nc.sync, planes2, stage2)
+
+        idle = psum.tile([P, P], F32, tag="z", bufs=3, name="idle")
+        for held, count in ((ones_codes, 16), (xq, 6), (wg, 6)):
+            for c in range(count):
+                nc.tensor.matmul_mx(
+                    out=idle[:], lhsT=held[:, 0:P].bitcast(FP8X4), lhsT_scale=ones_scale[:],
+                    rhs=ones_codes[:].bitcast(FP8X4), rhs_scale=ones_scale[:], start=True, stop=True,
+                )
 
         def plane1(a, cols):
             return planes1[:, a * W + cols.start : a * W + cols.stop]
@@ -115,9 +131,10 @@ def tile_mix_hidden_of_two_inputs_gated_kernel(
         def z_pass(i, s):
             if s == 0:
                 zsum[i] = psum.tile([P, W], F32, tag="z", bufs=3, name="zsum")
+            if s == 2:
                 x, xs, w, ws = xq, 0, wc[:], 2
             else:
-                x, xs, w, ws = xt[s - 1], 4 + s, wa[:, s - 1, :], 2 + s
+                x, xs, w, ws = xt[s], 5 + s, wa[:, s, :], 3 + s
             nc.tensor.matmul_mx(
                 out=zsum[i][:], lhsT=x[:, toks(i)].bitcast(FP8X4), lhsT_scale=plane1(xs, toks(i)),
                 rhs=w.bitcast(FP4X4), rhs_scale=plane1(ws, every), start=(s == 0), stop=(s == 2),
@@ -188,17 +205,16 @@ def tile_mix_hidden_of_two_inputs_gated_kernel(
         sigmoid(0)
         gate_pass(1)
         sigmoid(1)
-        z_pass(0, 0)
-        z_pass(1, 0)
         factor(0)
         factor(1)
+        z_pass(0, 0)
         z_pass(0, 1)
-        z_pass(0, 2)
-        hidden(0)
         gate_pass(2)
         sigmoid(2)
-        z_pass(1, 1)
-        z_pass(1, 2)
+        z_pass(0, 2)
+        hidden(0)
+        for s in range(3):
+            z_pass(1, s)
         hidden(1)
         gate_pass(3)
         sigmoid(3)

@@ -1,7 +1,6 @@
 from contextlib import ExitStack
 
 import concourse.mybir as mybir
-from concourse.masks import make_identity
 
 K, L, T, R, N = 1024, 512, 512, 512, 512
 FLOPS = 2 * T * (K * R + 2 * L * R + R * N + L * N)
@@ -28,7 +27,7 @@ def tile_mix_hidden_of_two_inputs_gated_kernel(
     with ExitStack() as ctx:
         keep = ctx.enter_context(tc.tile_pool(name="keep", bufs=1))
         work = ctx.enter_context(tc.tile_pool(name="work", bufs=4))
-        psum = ctx.enter_context(tc.psum_pool(name="psum", bufs=1))
+        psum = ctx.enter_context(tc.psum_pool(name="psum", bufs=8))
         ctx.enter_context(tc.manual_schedule())
 
         def load_rows(engine, stage, first, scales):
@@ -76,45 +75,60 @@ def tile_mix_hidden_of_two_inputs_gated_kernel(
         load_rows(nc.sync, stage1, 5, xt_scales)
         xq = load_fp8(xq_words[0], "xq", nc.scalar)
         wg = load_fp8(wg_words[0], "wg", nc.scalar)
-        xt_both = keep.tile([P, 2, W], I32, align_bytes=64)
-        nc.scalar.dma_start(out=xt_both[:], in_=xt_words.rearrange("z p c r -> p z (c r)").bitcast(I32))
-        xt = [xt_both[:, z, :] for z in range(2)]
+        nc.scalar.dma_start(out=us_col[:], in_=us.rearrange("(p j) o -> p (j o)", j=4))
 
-        nc.gpsimd.dma_start(out=us_col[:], in_=us.rearrange("(p j) o -> p (j o)", j=4))
-        make_identity(nc, ident[:])
         load_rows(nc.gpsimd, stage2, 0, wq_scales)
         load_rows(nc.gpsimd, stage2, 1, wb_scales)
 
+        step = keep.tile([P, P], F32, align_bytes=64)
+        column = keep.tile([P, P], F32, align_bytes=64)
+        folded = keep.tile([P, P], F32, align_bytes=64)
         nc.vector.memset(ones[:], 1.0)
+        nc.vector.memset(step[:], 1.0)
         nc.vector.memset(warm[:], 0.0)
         nc.vector.quantize_mx(out=ones_codes[:].bitcast(FP8X4), scales=ones_scale[:], in_=ones[:])
+        nc.vector.tensor_tensor_scan(
+            out=column[:], data0=step[:], data1=step[:], initial=-1.0, op0=ALU.mult, op1=ALU.add
+        )
         nc.vector.memset(planes1[:].bitcast(I32), 0)
+        nc.vector.transpose(out=folded[:], in_=column[:])
+        for q in range(4):
+            rows = slice(32 * q, 32 * q + 32)
+            nc.vector.tensor_scalar(
+                out=ident[rows, :], in0=column[rows, :], scalar1=folded[rows, 32 * q : 32 * q + 1], scalar2=None,
+                op0=ALU.is_equal,
+            )
         nc.vector.memset(planes2[:].bitcast(I32), 0)
         nc.scalar.activation(out=warm_out[:], in_=warm[:], func=ACT.Sigmoid)
         place_rows(nc.sync, planes1, stage1)
 
+        wc = load_fp4(wc_words[0], "wc")
         wa = keep.tile([P, 2, 2 * W], U8, align_bytes=64)
         nc.sync.dma_start(out=wa[:].bitcast(I32), in_=wa_words.rearrange("z p b -> p z b").bitcast(I32))
-        wc = load_fp4(wc_words[0], "wc")
+        xt = [load_fp8(xt_words[z], "xt%d" % z) for z in range(2)]
         wq = load_fp8(wq_words[0], "wq")
         wb = load_fp4(wb_words[0], "wb")
         place_rows(nc.sync, planes2, stage2)
 
-        idle = psum.tile([P, P], F32, tag="z", bufs=3, name="idle")
-        for held, count in ((ones_codes, 16), (xq, 6), (wg, 6)):
+        idle = psum.tile([P, P], F32, tag="bank", name="idle")
+
+        def keep_busy(held, count):
             for c in range(count):
                 nc.tensor.matmul_mx(
                     out=idle[:], lhsT=held[:, 0:P].bitcast(FP8X4), lhsT_scale=ones_scale[:],
                     rhs=ones_codes[:].bitcast(FP8X4), rhs_scale=ones_scale[:], start=True, stop=True,
                 )
 
+        keep_busy(ones_codes, 12)
+
         def plane1(a, cols):
             return planes1[:, a * W + cols.start : a * W + cols.stop]
 
         every = slice(0, W)
-        us_row = psum.tile([P, 4, P], F32, tag="o", bufs=3, name="us_row")
+        us_row = psum.tile([P, 4, P], F32, tag="bank", name="us_row")
         for j in range(4):
             nc.tensor.transpose(us_row[:, j, :], us_col[:, j : j + 1].to_broadcast([P, P]), ident[:])
+        keep_busy(wg, 8)
 
         gate, zsum, sig, fac, hid, turned, grouped, codes, cscale, acc = ({} for i in range(10))
 
@@ -122,7 +136,7 @@ def tile_mix_hidden_of_two_inputs_gated_kernel(
             return slice(i * P, (i + 1) * P)
 
         def gate_pass(i):
-            gate[i] = psum.tile([P, W], F32, tag="g", bufs=2, name="gate")
+            gate[i] = psum.tile([P, W], F32, tag="bank", name="gate")
             nc.tensor.matmul_mx(
                 out=gate[i][:], lhsT=xq[:, toks(i)].bitcast(FP8X4), lhsT_scale=plane1(0, toks(i)),
                 rhs=wg[:].bitcast(FP8X4), rhs_scale=plane1(1, every), start=True, stop=True,
@@ -130,11 +144,10 @@ def tile_mix_hidden_of_two_inputs_gated_kernel(
 
         def z_pass(i, s):
             if s == 0:
-                zsum[i] = psum.tile([P, W], F32, tag="z", bufs=3, name="zsum")
-            if s == 2:
+                zsum[i] = psum.tile([P, W], F32, tag="bank", name="zsum")
                 x, xs, w, ws = xq, 0, wc[:], 2
             else:
-                x, xs, w, ws = xt[s], 5 + s, wa[:, s, :], 3 + s
+                x, xs, w, ws = xt[s - 1], 4 + s, wa[:, s - 1, :], 2 + s
             nc.tensor.matmul_mx(
                 out=zsum[i][:], lhsT=x[:, toks(i)].bitcast(FP8X4), lhsT_scale=plane1(xs, toks(i)),
                 rhs=w.bitcast(FP4X4), rhs_scale=plane1(ws, every), start=(s == 0), stop=(s == 2),
@@ -159,7 +172,7 @@ def tile_mix_hidden_of_two_inputs_gated_kernel(
             )
 
         def turn(i):
-            turned[i] = psum.tile([P, 2, P], F32, tag="g", bufs=2, name="turned")
+            turned[i] = psum.tile([P, 2, P], F32, tag="bank", name="turned")
             pairs = hid[i][:].rearrange("t u p e -> t (u p e)").bitcast(F32)
             for u in range(2):
                 nc.tensor.transpose(turned[i][:, u, :], pairs[:, u * P : (u + 1) * P], ident[:])
@@ -176,8 +189,8 @@ def tile_mix_hidden_of_two_inputs_gated_kernel(
             cscale[i] = work.tile([P, P], U8, name="cscale", align_bytes=64)
             nc.vector.quantize_mx(out=codes[i][:].bitcast(FP8X4), scales=cscale[i][:], in_=grouped[i][:])
 
-        def skip_passes(i, rows, tag):
-            acc[i, rows] = psum.tile([P, len(rows), P], F32, tag=tag, bufs=3, name="acc")
+        def skip_passes(i, rows):
+            acc[i, rows] = psum.tile([P, len(rows), P], F32, tag="bank", name="acc")
             for b, a in enumerate(rows):
                 nc.tensor.matmul_mx(
                     out=acc[i, rows][:, b, :], lhsT=wq[:, toks(a)].bitcast(FP8X4), lhsT_scale=planes2[:, toks(a)],
@@ -193,64 +206,40 @@ def tile_mix_hidden_of_two_inputs_gated_kernel(
                 )
 
         def leave(i, rows, engine):
-            res = work.tile([P, len(rows), P], F32, name="res", bufs=5)
+            res = work.tile([P, len(rows), P], F32, name="res", bufs=8)
             if engine == "scalar":
                 nc.scalar.copy(out=res[:], in_=acc[i, rows][:])
             else:
                 nc.vector.tensor_copy(out=res[:], in_=acc[i, rows][:])
             dst = out.rearrange("(a p) t -> p a t", p=P)[:, rows[0] : rows[-1] + 1, toks(i)]
-            nc.sync.dma_start(out=dst, in_=res[:])
+            queue = nc.scalar if (i, rows) == (3, (2, 3)) else nc.sync
+            queue.dma_start(out=dst, in_=res[:])
 
-        gate_pass(0)
-        sigmoid(0)
-        gate_pass(1)
-        sigmoid(1)
+        def finish(i):
+            for half, rows in enumerate(((0, 1), (2, 3))):
+                skip_passes(i, rows)
+                second_passes(i, rows)
+                leave(i, rows, "scalar" if (half == 0) != (i == TILES - 1) else "vector")
+
+        for i in range(TILES):
+            gate_pass(i)
+            sigmoid(i)
         factor(0)
-        factor(1)
         z_pass(0, 0)
-        z_pass(0, 1)
-        gate_pass(2)
-        sigmoid(2)
-        z_pass(0, 2)
-        hidden(0)
-        for s in range(3):
-            z_pass(1, s)
-        hidden(1)
-        gate_pass(3)
-        sigmoid(3)
-        factor(2)
-        factor(3)
-        for s in range(3):
-            z_pass(2, s)
-        hidden(2)
-        turn(0)
-        regroup(0)
-        turn(1)
-        regroup(1)
-        quantise(0)
-        for s in range(3):
-            z_pass(3, s)
-        hidden(3)
-        quantise(1)
-        whole, low, high = (0, 1, 2, 3), (0, 1), (2, 3)
-        skip_passes(0, whole, "o")
-        second_passes(0, whole)
-        turn(2)
-        regroup(2)
-        turn(3)
-        regroup(3)
-        leave(0, whole, "scalar")
-        quantise(2)
-        quantise(3)
-        skip_passes(1, whole, "o")
-        second_passes(1, whole)
-        leave(1, whole, "vector")
-        skip_passes(2, whole, "o")
-        second_passes(2, whole)
-        leave(2, whole, "scalar")
-        skip_passes(3, low, "z")
-        second_passes(3, low)
-        leave(3, low, "vector")
-        skip_passes(3, high, "z")
-        second_passes(3, high)
-        leave(3, high, "scalar")
+        z_pass(1, 0)
+        for step_no in range(TILES + 4):
+            if step_no < TILES:
+                for s in range(1 if step_no < 2 else 0, 3):
+                    z_pass(step_no, s)
+                if step_no + 1 < TILES:
+                    factor(step_no + 1)
+                if step_no < TILES - 1:
+                    hidden(step_no)
+            if 0 <= step_no - 2 < TILES:
+                turn(step_no - 2)
+                regroup(step_no - 2)
+                if step_no == TILES - 1:
+                    hidden(step_no)
+                quantise(step_no - 2)
+            if 0 <= step_no - 4:
+                finish(step_no - 4)

from contextlib import ExitStack

import concourse.mybir as mybir

K, L, T, R, N = 1024, 512, 512, 512, 512
FLOPS = 2 * T * (K * R + 2 * L * R + R * N + L * N)

F32 = mybir.dt.float32
BF16 = mybir.dt.bfloat16
I32 = mybir.dt.int32
U8 = mybir.dt.uint8
FP8X4 = mybir.dt.float8_e4m3fn_x4
FP4X4 = mybir.dt.float4_e2m1fn_x4
ACT = mybir.ActivationFunctionType
ALU = mybir.AluOpType

P = 128
W = 512
TILES = T // P


def tile_mix_hidden_of_two_inputs_gated_kernel(
    tc, xt_words, xt_scales, wa_words, wa_scales, xq_words, xq_scales, wc_words, wc_scales,
    wg_words, wg_scales, us, wb_words, wb_scales, wq_words, wq_scales, out,
):
    nc = tc.nc
    with ExitStack() as ctx:
        keep = ctx.enter_context(tc.tile_pool(name="keep", bufs=1))
        work = ctx.enter_context(tc.tile_pool(name="work", bufs=4))
        psum = ctx.enter_context(tc.psum_pool(name="psum", bufs=8))
        ctx.enter_context(tc.manual_schedule())

        def load_rows(engine, stage, first, scales):
            passes = scales.shape[0]
            dst = stage[4:P:8, first * W : (first + passes) * W].bitcast(I32)
            engine.dma_start(
                out=dst.rearrange("q (z c) -> q z c", z=passes),
                in_=scales.rearrange("z q c -> q z c").bitcast(I32),
            )

        def place_rows(engine, planes, stage):
            for q in range(4):
                engine.dma_start(
                    out=planes[32 * q : 32 * q + 4, :].bitcast(I32),
                    in_=stage[32 * q + 4 : 32 * q + 32 : 8, :].bitcast(I32),
                )

        def load_fp8(words, name, engine=nc.sync):
            tl = keep.tile([P, W], I32, name=name, align_bytes=64)
            engine.dma_start(out=tl[:], in_=words.rearrange("p c r -> p (c r)").bitcast(I32))
            return tl

        def load_fp4(words, name):
            tl = keep.tile([P, 2 * W], U8, name=name, align_bytes=64)
            nc.sync.dma_start(out=tl[:].bitcast(I32), in_=words.bitcast(I32))
            return tl

        stage1 = keep.tile([P, 7 * W], U8, align_bytes=64)
        planes1 = keep.tile([P, 7 * W], U8, align_bytes=64)
        stage2 = keep.tile([P, 2 * W], U8, align_bytes=64)
        planes2 = keep.tile([P, 2 * W], U8, align_bytes=64)
        us_col = keep.tile([P, 4], F32)
        ident = keep.tile([P, P], F32, align_bytes=64)
        warm = keep.tile([P, 1], F32)
        warm_out = keep.tile([P, 1], F32)

        ones = keep.tile([P, 4 * P], BF16, align_bytes=64)
        ones_codes = keep.tile([P, P], I32, align_bytes=64)
        ones_scale = keep.tile([P, P], U8, align_bytes=64)

        load_rows(nc.sync, stage1, 0, xq_scales)
        load_rows(nc.scalar, stage1, 1, wg_scales)
        load_rows(nc.sync, stage1, 2, wc_scales)
        load_rows(nc.scalar, stage1, 3, wa_scales)
        load_rows(nc.sync, stage1, 5, xt_scales)
        xq = load_fp8(xq_words[0], "xq", nc.scalar)
        wg = load_fp8(wg_words[0], "wg", nc.scalar)
        nc.scalar.dma_start(out=us_col[:], in_=us.rearrange("(p j) o -> p (j o)", j=4))

        load_rows(nc.gpsimd, stage2, 0, wq_scales)
        load_rows(nc.gpsimd, stage2, 1, wb_scales)

        step = keep.tile([P, P], F32, align_bytes=64)
        column = keep.tile([P, P], F32, align_bytes=64)
        folded = keep.tile([P, P], F32, align_bytes=64)
        nc.vector.memset(ones[:], 1.0)
        nc.vector.memset(step[:], 1.0)
        nc.vector.memset(warm[:], 0.0)
        nc.vector.quantize_mx(out=ones_codes[:].bitcast(FP8X4), scales=ones_scale[:], in_=ones[:])
        nc.vector.tensor_tensor_scan(
            out=column[:], data0=step[:], data1=step[:], initial=-1.0, op0=ALU.mult, op1=ALU.add
        )
        nc.vector.memset(planes1[:].bitcast(I32), 0)
        nc.vector.transpose(out=folded[:], in_=column[:])
        for q in range(4):
            rows = slice(32 * q, 32 * q + 32)
            nc.vector.tensor_scalar(
                out=ident[rows, :], in0=column[rows, :], scalar1=folded[rows, 32 * q : 32 * q + 1], scalar2=None,
                op0=ALU.is_equal,
            )
        nc.vector.memset(planes2[:].bitcast(I32), 0)
        nc.scalar.activation(out=warm_out[:], in_=warm[:], func=ACT.Sigmoid)
        place_rows(nc.sync, planes1, stage1)

        wc = load_fp4(wc_words[0], "wc")
        wa = keep.tile([P, 2, 2 * W], U8, align_bytes=64)
        nc.sync.dma_start(out=wa[:].bitcast(I32), in_=wa_words.rearrange("z p b -> p z b").bitcast(I32))
        xt = [load_fp8(xt_words[z], "xt%d" % z) for z in range(2)]
        wq = load_fp8(wq_words[0], "wq")
        wb = load_fp4(wb_words[0], "wb")
        place_rows(nc.sync, planes2, stage2)

        idle = psum.tile([P, P], F32, tag="bank", name="idle")

        def keep_busy(held, count):
            for c in range(count):
                nc.tensor.matmul_mx(
                    out=idle[:], lhsT=held[:, 0:P].bitcast(FP8X4), lhsT_scale=ones_scale[:],
                    rhs=ones_codes[:].bitcast(FP8X4), rhs_scale=ones_scale[:], start=True, stop=True,
                )

        keep_busy(ones_codes, 12)

        def plane1(a, cols):
            return planes1[:, a * W + cols.start : a * W + cols.stop]

        every = slice(0, W)
        us_row = psum.tile([P, 4, P], F32, tag="bank", name="us_row")
        for j in range(4):
            nc.tensor.transpose(us_row[:, j, :], us_col[:, j : j + 1].to_broadcast([P, P]), ident[:])
        keep_busy(wg, 8)

        gate, zsum, sig, fac, hid, turned, grouped, codes, cscale, acc = ({} for i in range(10))

        def toks(i):
            return slice(i * P, (i + 1) * P)

        def gate_pass(i):
            gate[i] = psum.tile([P, W], F32, tag="bank", name="gate")
            nc.tensor.matmul_mx(
                out=gate[i][:], lhsT=xq[:, toks(i)].bitcast(FP8X4), lhsT_scale=plane1(0, toks(i)),
                rhs=wg[:].bitcast(FP8X4), rhs_scale=plane1(1, every), start=True, stop=True,
            )

        def z_pass(i, s):
            if s == 0:
                zsum[i] = psum.tile([P, W], F32, tag="bank", name="zsum")
                x, xs, w, ws = xq, 0, wc[:], 2
            else:
                x, xs, w, ws = xt[s - 1], 4 + s, wa[:, s - 1, :], 2 + s
            nc.tensor.matmul_mx(
                out=zsum[i][:], lhsT=x[:, toks(i)].bitcast(FP8X4), lhsT_scale=plane1(xs, toks(i)),
                rhs=w.bitcast(FP4X4), rhs_scale=plane1(ws, every), start=(s == 0), stop=(s == 2),
            )

        def sigmoid(i):
            sig[i] = work.tile([P, 2, P, 2], F32, name="sig")
            nc.scalar.activation(
                out=sig[i][:], in_=gate[i][:].rearrange("t (p u e) -> t u p e", u=2, e=2), func=ACT.Sigmoid
            )

        def factor(i):
            fac[i] = work.tile([P, 2, P, 2], F32, name="fac")
            nc.vector.tensor_tensor(
                out=fac[i][:], in0=sig[i][:], in1=us_row[:].rearrange("t (u e) p -> t u p e", e=2), op=ALU.mult
            )

        def hidden(i):
            hid[i] = work.tile([P, 2, P, 2], BF16, name="hid", align_bytes=64)
            nc.vector.tensor_tensor(
                out=hid[i][:], in0=zsum[i][:].rearrange("t (p u e) -> t u p e", u=2, e=2), in1=fac[i][:], op=ALU.mult
            )

        def turn(i):
            turned[i] = psum.tile([P, 2, P], F32, tag="bank", name="turned")
            pairs = hid[i][:].rearrange("t u p e -> t (u p e)").bitcast(F32)
            for u in range(2):
                nc.tensor.transpose(turned[i][:, u, :], pairs[:, u * P : (u + 1) * P], ident[:])

        def regroup(i):
            grouped[i] = work.tile([P, 4 * P], BF16, name="grouped", align_bytes=64)
            nc.scalar.copy(
                out=grouped[i][:].bitcast(F32).rearrange("p (t u) -> p t u", u=2),
                in_=turned[i][:].rearrange("p u t -> p t u"),
            )

        def quantise(i):
            codes[i] = work.tile([P, P], I32, name="codes", align_bytes=64)
            cscale[i] = work.tile([P, P], U8, name="cscale", align_bytes=64)
            nc.vector.quantize_mx(out=codes[i][:].bitcast(FP8X4), scales=cscale[i][:], in_=grouped[i][:])

        def skip_passes(i, rows):
            acc[i, rows] = psum.tile([P, len(rows), P], F32, tag="bank", name="acc")
            for b, a in enumerate(rows):
                nc.tensor.matmul_mx(
                    out=acc[i, rows][:, b, :], lhsT=wq[:, toks(a)].bitcast(FP8X4), lhsT_scale=planes2[:, toks(a)],
                    rhs=xq[:, toks(i)].bitcast(FP8X4), rhs_scale=plane1(0, toks(i)), start=(b == 0), stop=False,
                )

        def second_passes(i, rows):
            for b, a in enumerate(rows):
                nc.tensor.matmul_mx(
                    out=acc[i, rows][:, b, :], lhsT=wb[:, 2 * a * P : 2 * (a + 1) * P].bitcast(FP4X4),
                    lhsT_scale=planes2[:, W + a * P : W + (a + 1) * P],
                    rhs=codes[i][:].bitcast(FP8X4), rhs_scale=cscale[i][:], start=False, stop=(b == len(rows) - 1),
                )

        def leave(i, rows, engine):
            res = work.tile([P, len(rows), P], F32, name="res", bufs=8)
            if engine == "scalar":
                nc.scalar.copy(out=res[:], in_=acc[i, rows][:])
            else:
                nc.vector.tensor_copy(out=res[:], in_=acc[i, rows][:])
            dst = out.rearrange("(a p) t -> p a t", p=P)[:, rows[0] : rows[-1] + 1, toks(i)]
            queue = nc.scalar if (i, rows) == (3, (2, 3)) else nc.sync
            queue.dma_start(out=dst, in_=res[:])

        def finish(i):
            for half, rows in enumerate(((0, 1), (2, 3))):
                skip_passes(i, rows)
                second_passes(i, rows)
                leave(i, rows, "scalar" if (half == 0) != (i == TILES - 1) else "vector")

        for i in range(TILES):
            gate_pass(i)
            sigmoid(i)
        factor(0)
        z_pass(0, 0)
        z_pass(1, 0)
        for step_no in range(TILES + 4):
            if step_no < TILES:
                for s in range(1 if step_no < 2 else 0, 3):
                    z_pass(step_no, s)
                if step_no + 1 < TILES:
                    factor(step_no + 1)
                if step_no < TILES - 1:
                    hidden(step_no)
            if 0 <= step_no - 2 < TILES:
                turn(step_no - 2)
                regroup(step_no - 2)
                if step_no == TILES - 1:
                    hidden(step_no)
                quantise(step_no - 2)
            if 0 <= step_no - 4:
                finish(step_no - 4)
